import numpy as np
import ml_dtypes


def mxq(x, axis, fmt="e4m3"):
    dtype, down = {"e4m3": (ml_dtypes.float8_e4m3fn, 7), "e5m2": (ml_dtypes.float8_e5m2, 14)}[fmt]
    v = np.moveaxis(np.asarray(x, np.float32).astype(ml_dtypes.bfloat16).astype(np.float64), axis, -1)
    blocks = v.reshape(v.shape[:-1] + (-1, 32))
    amax = np.abs(blocks).max(-1, keepdims=True)
    byte = np.maximum(np.where(amax > 0, np.frexp(amax)[1] - 1 + 127, 0) - down, 1)
    scale = np.exp2(byte - 127.0)
    codes = (blocks / scale).astype(np.float32).astype(dtype).astype(np.float64)
    return np.moveaxis((codes * scale).reshape(v.shape), -1, axis)


WIDE = False


def mx_kscale(k):
    if not WIDE:
        return np.ones(k)
    levels = np.array([10, -10, 5, -5, 0])
    if k % 512:
        return np.exp2(np.random.permutation(np.resize(levels, k // 32))).repeat(32)
    a = np.empty((k // 512, 16))
    for p in range(k // 512):
        a[p, :8] = np.random.permutation(np.resize(levels, 8))
        for g in range(8):
            far = levels[np.abs(levels - a[p, g]) >= 10]
            a[p, g + 8] = far[np.random.randint(len(far))]
    return np.exp2(a.ravel()).repeat(32)


def f64(x):
    return np.asarray(x).astype(np.float64)


def striped(idx):
    return np.tile(idx.reshape(-1, 16).T, (8, 1)).astype(np.uint16)


def unstriped(offs):
    return offs[:16].T.reshape(-1).astype(np.int64)


def pack_weight(w):
    k, n = w.shape
    w = f64(np.asarray(w, np.float32).astype(ml_dtypes.bfloat16)).reshape(k // 32, 32, n)
    amax = np.abs(w).max(1)
    byte = np.clip(np.where(amax > 0, np.frexp(amax)[1] - 1 + 127 - 7, 1), 1, 254)
    scaled = (w * np.exp2(127.0 - byte)[:, None, :]).reshape(k, n).astype(np.float32)
    words = np.ascontiguousarray(scaled.reshape(k // 512, 128, 4, n).transpose(0, 1, 3, 2)).astype(ml_dtypes.float8_e4m3fn).view(np.uint8)
    return words, np.ascontiguousarray(byte.astype(np.uint8).reshape(k // 512, 16, n))


def unpack_weight(words, scales):
    g, p, n, _ = words.shape
    vals = np.ascontiguousarray(words).view(ml_dtypes.float8_e4m3fn).astype(np.float64) * np.repeat(np.exp2(scales.astype(np.float64) - 127.0), 8, axis=1)[..., None]
    return vals.transpose(0, 1, 3, 2).reshape(g * 512, n)


def sigmoid(v):
    return 1.0 / (1.0 + np.exp(-np.maximum(v, -700.0)))


H, K, T, S, D, N = 512, 1024, 4096, 1024, 4, 128
P = 2 ** 7


def setup_inputs():
    n = np.random.standard_normal
    s = mx_kscale(K)[:, None]
    u = mx_kscale(H)
    packed_xT = pack_weight(n((K, T)) * s)
    return {
        "x_words": packed_xT[0],
        "x_scales": packed_xT[1],
        "w1": (n((K, H)) / np.sqrt(K) / s).astype(np.float32),
        "logt": (np.tile(n(S), (P, 1))).astype(np.float32),
        "unit": (np.random.uniform(0.5, 1.5, (H, 1)) * u[:, None]).astype(np.float32),
        "wo": (n((H, N)) / np.sqrt(H) / u[:, None]).astype(np.float32),
        "offs": striped(np.random.permutation(T)[:S]),
    }


def reference(x_words, x_scales, w1, logt, unit, wo, offs):
    xq = unpack_weight(x_words, x_scales)[:, unstriped(offs)]
    y = mxq(f64(w1), 0, "e4m3").T @ xq
    px = sigmoid(y)
    hat = px * (-1.0 * px + 1.0) + 0.02
    lr = y - f64(logt)[:1]
    wl = hat * lr
    den = hat.reshape(len(hat), -1, D).sum(axis=2)
    rad = (wl.reshape(len(wl), -1, D).sum(axis=2)) / den
    wv = hat * ((lr - np.repeat(rad, D, axis=1)) ** 2)
    unc = np.tanh(rad) * (np.sqrt((wv.reshape(len(wv), -1, D).sum(axis=2)) / den))
    zz = f64(unit) * unc
    return mxq(f64(wo), 0, "e4m3").T @ mxq(zz, 0, "e4m3")

@@ -1,0 +1,203 @@
+from contextlib import ExitStack
+
+import concourse.mybir as mybir
+from concourse.masks import make_identity
+
+H, K, T, S, D, N = 512, 1024, 4096, 1024, 4, 128
+FLOPS = 2 * K * H * S + 2 * H * N * (S // D)
+
+F32 = mybir.dt.float32
+BF16 = mybir.dt.bfloat16
+I32 = mybir.dt.int32
+U32 = mybir.dt.uint32
+U16 = mybir.dt.uint16
+U8 = mybir.dt.uint8
+FP8X4 = mybir.dt.float8_e4m3fn_x4
+ACT = mybir.ActivationFunctionType
+ALU = mybir.AluOpType
+
+P = 128
+PACK = 4
+PASSES = K // (P * PACK)
+BLOCKS = S // (D * P)
+ENTRIES = D * P
+TANH_GAIN = 2.5
+PEAK = 6.75
+
+
+def tile_picked_yhdrmg_dev_p_kernel(tc, x_words, x_scales, w1, logt, unit, wo, offs, out):
+    nc = tc.nc
+    with ExitStack() as ctx:
+        keep = ctx.enter_context(tc.tile_pool(name="keep", bufs=1))
+        psum = ctx.enter_context(tc.psum_pool(name="psum", bufs=1))
+
+        def sbuf(name, shape, dtype, tag=None):
+            return keep.tile(shape, dtype, name=name, tag=tag or name, align_bytes=64)
+
+        def bank(name, index, shape):
+            return psum.tile(shape, F32, name=name, tag="bank%d" % index)
+
+        offsets = keep.tile([P, S // 16], U16, name="offsets")
+        nc.sync.dma_start(offsets[:], offs)
+        scale_rows = sbuf("scale_rows", [P, T], U8)
+        nc.sync.dma_start(out=scale_rows[0:32, :].bitcast(I32), in_=x_scales.rearrange("o q c -> (o q) c").bitcast(I32))
+        nc.vector.memset(scale_rows[32:64, :].bitcast(I32), 0)
+        nc.vector.memset(scale_rows[64:128, :].bitcast(I32), 0)
+        log_time = sbuf("log_time", [P, BLOCKS, D], F32)
+        nc.sync.dma_start(out=log_time[:], in_=logt[0].rearrange("(b p d) -> p b d", b=BLOCKS, d=D))
+        unit_sb = sbuf("unit_sb", [P, PACK], F32)
+        nc.sync.dma_start(out=unit_sb[:], in_=unit.rearrange("(p t) o -> p (t o)", t=PACK))
+        w1_raw = []
+        for g in range(PASSES):
+            raw = sbuf("w1_raw%d" % g, [P, PACK, H], F32)
+            nc.sync.dma_start(out=raw[:], in_=w1[g * P * PACK:(g + 1) * P * PACK, :].rearrange("(p j) n -> p j n", j=PACK))
+            w1_raw.append(raw)
+        wo_raw = sbuf("wo_raw", [P, PACK, N], F32)
+        nc.sync.dma_start(out=wo_raw[:], in_=wo.rearrange("(p j) n -> p j n", j=PACK))
+        tables = []
+        for g in range(PASSES):
+            table = sbuf("table%d" % g, [P, T], U32)
+            nc.sync.dma_start(out=table[:].bitcast(I32), in_=x_words[g].rearrange("p n t -> p (n t)").bitcast(I32))
+            tables.append(table)
+
+        identity = sbuf("identity", [P, P], F32)
+        make_identity(nc, identity[:])
+
+        picked_rows = sbuf("picked_rows", [P, S], U8)
+        nc.vector.tensor_copy(out=picked_rows[:], in_=scale_rows[:].indirect(offsets[:]))
+        dealt_rows = sbuf("dealt_rows", [P, S], U8)
+        nc.vector.tensor_copy(
+            out=dealt_rows[:].rearrange("p (b d v) -> p b d v", b=BLOCKS, d=D),
+            in_=picked_rows[:].rearrange("p (b v d) -> p b d v", b=BLOCKS, d=D),
+        )
+        x_planes = sbuf("x_planes", [P, S], U8)
+        nc.vector.memset(x_planes[:].bitcast(I32), 0)
+        for g in range(PASSES):
+            for q in range(4):
+                src = 16 * g + 4 * q
+                dst = 32 * q + 4 * g
+                queue = nc.scalar if g == 0 else nc.gpsimd
+                queue.dma_start(out=x_planes[dst:dst + 4, :].bitcast(I32), in_=dealt_rows[src:src + 4, :].bitcast(I32))
+
+        def quantise_weight(name, raw, width):
+            grouped = sbuf(name + "_bf", [P, width, PACK], BF16)
+            nc.scalar.activation(
+                out=grouped[:].rearrange("p (c i) j -> p c j i", i=4),
+                in_=raw[:].rearrange("p j (c i) -> p c j i", i=4),
+                func=ACT.Copy,
+            )
+            codes = sbuf(name + "_codes", [P, width], U32)
+            plane = sbuf(name + "_plane", [P, width], U8)
+            nc.vector.quantize_mx(out=codes[:].bitcast(FP8X4), scales=plane[:], in_=grouped[:].rearrange("p c j -> p (c j)"))
+            return codes, plane
+
+        w1_q = [quantise_weight("w1_%d" % g, w1_raw[g], H) for g in range(PASSES)]
+        wo_codes, wo_plane = quantise_weight("wo", wo_raw, N)
+
+        y = [[bank("y%d_%d" % (b, d), D * b + d, [P, H]) for d in range(D)] for b in range(BLOCKS)]
+        for g in range(PASSES):
+            for b in range(BLOCKS):
+                picked = sbuf("picked%d_%d" % (g, b), [P, D, P], U32)
+                cols = ENTRIES // 16
+                nc.vector.tensor_copy(
+                    out=picked[:].rearrange("p d v -> p v d"),
+                    in_=tables[g][:].indirect(offsets[:, b * cols:(b + 1) * cols]),
+                )
+                for d in range(D):
+                    first = b * ENTRIES + d * P
+                    nc.tensor.matmul_mx(
+                        out=y[b][d][:],
+                        lhsT=picked[:, d, :].bitcast(FP8X4),
+                        lhsT_scale=x_planes[4 * g:P, first:first + P],
+                        rhs=w1_q[g][0][:].bitcast(FP8X4),
+                        rhs_scale=w1_q[g][1][:],
+                        start=(g == 0),
+                        stop=(g == PASSES - 1),
+                    )
+
+        def turned_add(total, term, start, stop):
+            for t in range(PACK):
+                nc.tensor.matmul(
+                    total[:, t, :], lhsT=term[:, t, :], rhs=identity[:],
+                    start=(start and t == 0), stop=(stop and t == PACK - 1), is_transpose=True,
+                )
+
+        sums = []
+        for b in range(BLOCKS):
+            yb = [y[b][d][:].rearrange("p (m t) -> p t m", t=PACK) for d in range(D)]
+            pairs = [sbuf("tanh%d_%d" % (b, u), [P, 2, PACK, P], F32) for u in range(2)]
+            th = [pairs[d // 2][:, d % 2] for d in range(D)]
+            sq = [sbuf("sq%d_%d" % (b, d), [P, PACK, P], F32) for d in range(D)]
+            base = sbuf("base%d" % b, [P, PACK, P], F32)
+            nc.vector.tensor_scalar(out=base[:], in0=yb[0], scalar1=log_time[:, b, 0:1], scalar2=None, op0=ALU.subtract)
+            firsts, seconds = [], []
+            for d in range(1, D):
+                nc.scalar.activation(out=th[d], in_=yb[d], func=ACT.Tanh, scale=0.5)
+                nc.scalar.activation(out=sq[d][:], in_=th[d], func=ACT.Square, scale=TANH_GAIN)
+                dev = sbuf("dev%d_%d" % (b, d), [P, PACK, P], F32)
+                nc.vector.scalar_tensor_tensor(
+                    out=dev[:], in0=yb[d], scalar=log_time[:, b, d:d + 1], in1=base[:], op0=ALU.subtract, op1=ALU.subtract)
+                if d == 1:
+                    nc.scalar.activation(out=th[0], in_=yb[0], func=ACT.Tanh, scale=0.5)
+                m1 = sbuf("first%d_%d" % (b, d), [P, PACK, P], F32)
+                nc.vector.scalar_tensor_tensor(
+                    out=m1[:], in0=sq[d][:], scalar=PEAK, in1=dev[:], op0=ALU.subtract, op1=ALU.mult)
+                m2 = sbuf("second%d_%d" % (b, d), [P, PACK, P], F32)
+                nc.vector.tensor_tensor(out=m2[:], in0=m1[:], in1=dev[:], op=ALU.mult)
+                if d == 1:
+                    nc.vector.scalar_tensor_tensor(
+                        out=sq[0][:], in0=th[0], scalar=TANH_GAIN * TANH_GAIN, in1=th[0], op0=ALU.mult, op1=ALU.mult)
+                firsts.append(m1)
+                seconds.append(m2)
+            sq_sum = bank("sq_sum%d" % b, D * b, [P, PACK, P])
+            for n, d in enumerate((1, 0, 2, 3)):
+                turned_add(sq_sum, sq[d], n == 0, n == D - 1)
+            base_t = bank("base_t%d" % b, D * b + 1, [P, PACK, P])
+            turned_add(base_t, base, True, True)
+            first_sum = bank("first_sum%d" % b, D * b + 2, [P, PACK, P])
+            second_sum = bank("second_sum%d" % b, D * b + 3, [P, PACK, P])
+            for n in range(D - 1):
+                turned_add(first_sum, firsts[n], n == 0, n == D - 2)
+            for n in range(D - 1):
+                turned_add(second_sum, seconds[n], n == 0, n == D - 2)
+            sums.append([tile[:].rearrange("p t v -> p v t") for tile in (sq_sum, base_t, first_sum, second_sum)])
+
+        shape = [P, BLOCKS, P, PACK]
+        log_den = sbuf("log_den", shape, F32, tag="tanh%d_1" % (BLOCKS - 1))
+        for b in range(BLOCKS):
+            nc.scalar.activation(out=log_den[:, b], in_=sums[b][0], func=ACT.Ln, scale=-1.0, bias=D * PEAK - 1.0)
+        recip = sbuf("recip", shape, F32)
+        nc.scalar.activation(out=recip[:], in_=log_den[:], func=ACT.Sigmoid, scale=-1.0)
+        mean = sbuf("mean", shape, F32)
+        rad = sbuf("rad", shape, F32)
+        mean_sq = sbuf("mean_sq", shape, F32)
+        for b in range(BLOCKS):
+            nc.vector.scalar_tensor_tensor(out=mean[:, b], in0=sums[b][2], scalar=-1.0, in1=recip[:, b], op0=ALU.mult, op1=ALU.mult)
+            nc.vector.tensor_tensor(out=rad[:, b], in0=sums[b][1], in1=mean[:, b], op=ALU.add)
+            nc.scalar.activation(out=mean_sq[:, b], in_=mean[:, b], func=ACT.Square)
+        bounded = sbuf("bounded", shape, F32)
+        nc.scalar.activation(out=bounded[:], in_=rad[:], func=ACT.Tanh)
+        raw_second = sbuf("raw_second", shape, F32)
+        var = sbuf("var", shape, F32)
+        for b in range(BLOCKS):
+            nc.vector.scalar_tensor_tensor(out=raw_second[:, b], in0=sums[b][3], scalar=-1.0, in1=recip[:, b], op0=ALU.mult, op1=ALU.mult)
+            nc.vector.tensor_tensor(out=var[:, b], in0=raw_second[:, b], in1=mean_sq[:, b], op=ALU.subtract)
+        gained = sbuf("gained", shape, F32)
+        spread = sbuf("spread", shape, F32, tag="rad")
+        for b in range(BLOCKS):
+            nc.vector.tensor_tensor(
+                out=gained[:, b], in0=bounded[:, b], in1=unit_sb[:].unsqueeze(1).to_broadcast([P, P, PACK]), op=ALU.mult)
+            nc.scalar.activation(out=spread[:, b], in_=var[:, b], func=ACT.Sqrt)
+        for b in range(BLOCKS):
+            zz = sbuf("zz%d" % b, [P, P, PACK], BF16)
+            nc.vector.tensor_tensor(out=zz[:], in0=gained[:, b], in1=spread[:, b], op=ALU.mult)
+            z_codes = sbuf("z_codes%d" % b, [P, P], U32)
+            z_plane = sbuf("z_plane%d" % b, [P, P], U8)
+            nc.vector.quantize_mx(out=z_codes[:].bitcast(FP8X4), scales=z_plane[:], in_=zz[:].rearrange("p v t -> p (v t)"))
+            acc = bank("acc%d" % b, D * b, [P, P])
+            nc.tensor.matmul_mx(
+                out=acc[:], lhsT=wo_codes[:].bitcast(FP8X4), lhsT_scale=wo_plane[:],
+                rhs=z_codes[:].bitcast(FP8X4), rhs_scale=z_plane[:], start=True, stop=True)
+            result = sbuf("result%d" % b, [P, P], F32)
+            nc.scalar.copy(out=result[:], in_=acc[:])
+            nc.sync.dma_start(out=out[:, b * P:(b + 1) * P], in_=result[:])

@@ -52,13 +52,13 @@ def tile_picked_yhdrmg_dev_p_kernel(tc, x_words, x_scales, w1, logt, unit, wo, o
             raw = sbuf("w1_raw%d" % g, [P, PACK, H], F32)
             nc.sync.dma_start(out=raw[:], in_=w1[g * P * PACK:(g + 1) * P * PACK, :].rearrange("(p j) n -> p j n", j=PACK))
             w1_raw.append(raw)
-        wo_raw = sbuf("wo_raw", [P, PACK, N], F32)
-        nc.sync.dma_start(out=wo_raw[:], in_=wo.rearrange("(p j) n -> p j n", j=PACK))
         tables = []
         for g in range(PASSES):
             table = sbuf("table%d" % g, [P, T], U32)
             nc.sync.dma_start(out=table[:].bitcast(I32), in_=x_words[g].rearrange("p n t -> p (n t)").bitcast(I32))
             tables.append(table)
+        wo_raw = sbuf("wo_raw", [P, PACK, N], F32)
+        nc.sync.dma_start(out=wo_raw[:], in_=wo.rearrange("(p j) n -> p j n", j=PACK))
 
         identity = sbuf("identity", [P, P], F32)
         make_identity(nc, identity[:])
@@ -76,23 +76,19 @@ def tile_picked_yhdrmg_dev_p_kernel(tc, x_words, x_scales, w1, logt, unit, wo, o
             for q in range(4):
                 src = 16 * g + 4 * q
                 dst = 32 * q + 4 * g
-                queue = nc.scalar if g == 0 else nc.gpsimd
+                queue = nc.scalar if 4 * g + q < 5 else nc.gpsimd
                 queue.dma_start(out=x_planes[dst:dst + 4, :].bitcast(I32), in_=dealt_rows[src:src + 4, :].bitcast(I32))
 
-        def quantise_weight(name, raw, width):
+        def quantise_weight(name, raw, width, out_order, in_order):
             grouped = sbuf(name + "_bf", [P, width, PACK], BF16)
             nc.scalar.activation(
-                out=grouped[:].rearrange("p (c i) j -> p c j i", i=4),
-                in_=raw[:].rearrange("p j (c i) -> p c j i", i=4),
-                func=ACT.Copy,
-            )
+                out=grouped[:].rearrange(out_order, i=PACK), in_=raw[:].rearrange(in_order, i=PACK), func=ACT.Copy)
             codes = sbuf(name + "_codes", [P, width], U32)
             plane = sbuf(name + "_plane", [P, width], U8)
             nc.vector.quantize_mx(out=codes[:].bitcast(FP8X4), scales=plane[:], in_=grouped[:].rearrange("p c j -> p (c j)"))
             return codes, plane
 
-        w1_q = [quantise_weight("w1_%d" % g, w1_raw[g], H) for g in range(PASSES)]
-        wo_codes, wo_plane = quantise_weight("wo", wo_raw, N)
+        w1_q = [quantise_weight("w1_%d" % g, w1_raw[g], H, "p (i c) j -> p c i j", "p j (c i) -> p c i j") for g in range(PASSES)]
 
         y = [[bank("y%d_%d" % (b, d), D * b + d, [P, H]) for d in range(D)] for b in range(BLOCKS)]
         for g in range(PASSES):
@@ -115,6 +111,8 @@ def tile_picked_yhdrmg_dev_p_kernel(tc, x_words, x_scales, w1, logt, unit, wo, o
                         stop=(g == PASSES - 1),
                     )
 
+        wo_codes, wo_plane = quantise_weight("wo", wo_raw, N, "p (c i) j -> p c j i", "p j (c i) -> p c j i")
+
         def turned_add(total, term, start, stop):
             for t in range(PACK):
                 nc.tensor.matmul(
@@ -124,7 +122,7 @@ def tile_picked_yhdrmg_dev_p_kernel(tc, x_words, x_scales, w1, logt, unit, wo, o
 
         sums = []
         for b in range(BLOCKS):
-            yb = [y[b][d][:].rearrange("p (m t) -> p t m", t=PACK) for d in range(D)]
+            yb = [y[b][d][:].rearrange("p (t m) -> p t m", t=PACK) for d in range(D)]
             pairs = [sbuf("tanh%d_%d" % (b, u), [P, 2, PACK, P], F32) for u in range(2)]
             th = [pairs[d // 2][:, d % 2] for d in range(D)]
             sq = [sbuf("sq%d_%d" % (b, d), [P, PACK, P], F32) for d in range(D)]
@@ -168,29 +166,34 @@ def tile_picked_yhdrmg_dev_p_kernel(tc, x_words, x_scales, w1, logt, unit, wo, o
             nc.scalar.activation(out=log_den[:, b], in_=sums[b][0], func=ACT.Ln, scale=-1.0, bias=D * PEAK - 1.0)
         recip = sbuf("recip", shape, F32)
         nc.scalar.activation(out=recip[:], in_=log_den[:], func=ACT.Sigmoid, scale=-1.0)
-        mean = sbuf("mean", shape, F32)
-        rad = sbuf("rad", shape, F32)
-        mean_sq = sbuf("mean_sq", shape, F32)
+        half = [P, P, PACK]
+        means, mean_sqs, bounded = [], [], []
         for b in range(BLOCKS):
-            nc.vector.scalar_tensor_tensor(out=mean[:, b], in0=sums[b][2], scalar=-1.0, in1=recip[:, b], op0=ALU.mult, op1=ALU.mult)
-            nc.vector.tensor_tensor(out=rad[:, b], in0=sums[b][1], in1=mean[:, b], op=ALU.add)
-            nc.scalar.activation(out=mean_sq[:, b], in_=mean[:, b], func=ACT.Square)
-        bounded = sbuf("bounded", shape, F32)
-        nc.scalar.activation(out=bounded[:], in_=rad[:], func=ACT.Tanh)
-        raw_second = sbuf("raw_second", shape, F32)
-        var = sbuf("var", shape, F32)
+            mean = sbuf("mean%d" % b, half, F32)
+            nc.vector.scalar_tensor_tensor(out=mean[:], in0=sums[b][2], scalar=-1.0, in1=recip[:, b], op0=ALU.mult, op1=ALU.mult)
+            rad = sbuf("rad%d" % b, half, F32)
+            nc.vector.tensor_tensor(out=rad[:], in0=sums[b][1], in1=mean[:], op=ALU.add)
+            mean_sq = sbuf("mean_sq%d" % b, half, F32)
+            nc.scalar.activation(out=mean_sq[:], in_=mean[:], func=ACT.Square)
+            bound = sbuf("bounded%d" % b, half, F32)
+            nc.scalar.activation(out=bound[:], in_=rad[:], func=ACT.Tanh)
+            mean_sqs.append(mean_sq)
+            bounded.append(bound)
+        variances = []
         for b in range(BLOCKS):
-            nc.vector.scalar_tensor_tensor(out=raw_second[:, b], in0=sums[b][3], scalar=-1.0, in1=recip[:, b], op0=ALU.mult, op1=ALU.mult)
-            nc.vector.tensor_tensor(out=var[:, b], in0=raw_second[:, b], in1=mean_sq[:, b], op=ALU.subtract)
-        gained = sbuf("gained", shape, F32)
-        spread = sbuf("spread", shape, F32, tag="rad")
+            raw_second = sbuf("raw_second%d" % b, half, F32)
+            nc.vector.scalar_tensor_tensor(out=raw_second[:], in0=sums[b][3], scalar=-1.0, in1=recip[:, b], op0=ALU.mult, op1=ALU.mult)
+            var = sbuf("var%d" % b, half, F32)
+            nc.vector.tensor_tensor(out=var[:], in0=raw_second[:], in1=mean_sqs[b][:], op=ALU.subtract)
+            variances.append(var)
         for b in range(BLOCKS):
+            gained = sbuf("gained%d" % b, half, F32)
             nc.vector.tensor_tensor(
-                out=gained[:, b], in0=bounded[:, b], in1=unit_sb[:].unsqueeze(1).to_broadcast([P, P, PACK]), op=ALU.mult)
-            nc.scalar.activation(out=spread[:, b], in_=var[:, b], func=ACT.Sqrt)
-        for b in range(BLOCKS):
-            zz = sbuf("zz%d" % b, [P, P, PACK], BF16)
-            nc.vector.tensor_tensor(out=zz[:], in0=gained[:, b], in1=spread[:, b], op=ALU.mult)
+                out=gained[:], in0=bounded[b][:], in1=unit_sb[:].unsqueeze(1).to_broadcast(half), op=ALU.mult)
+            spread = sbuf("spread%d" % b, half, F32, tag="rad%d" % (BLOCKS - 1 - b))
+            nc.scalar.activation(out=spread[:], in_=variances[b][:], func=ACT.Sqrt)
+            zz = sbuf("zz%d" % b, half, BF16)
+            nc.vector.tensor_tensor(out=zz[:], in0=gained[:], in1=spread[:], op=ALU.mult)
             z_codes = sbuf("z_codes%d" % b, [P, P], U32)
             z_plane = sbuf("z_plane%d" % b, [P, P], U8)
             nc.vector.quantize_mx(out=z_codes[:].bitcast(FP8X4), scales=z_plane[:], in_=zz[:].rearrange("p v t -> p (v t)"))

@@ -44,51 +44,60 @@ def tile_picked_yhdrmg_dev_p_kernel(tc, x_words, x_scales, w1, logt, unit, wo, o
         nc.vector.memset(scale_rows[32:64, :].bitcast(I32), 0)
         nc.vector.memset(scale_rows[64:128, :].bitcast(I32), 0)
         log_time = sbuf("log_time", [P, BLOCKS, D], F32)
-        nc.sync.dma_start(out=log_time[:], in_=logt[0].rearrange("(b p d) -> p b d", b=BLOCKS, d=D))
+        nc.gpsimd.dma_start(out=log_time[:], in_=logt[0].rearrange("(b p d) -> p b d", b=BLOCKS, d=D))
         unit_sb = sbuf("unit_sb", [P, PACK], F32)
-        nc.sync.dma_start(out=unit_sb[:], in_=unit.rearrange("(p t) o -> p (t o)", t=PACK))
+        nc.gpsimd.dma_start(out=unit_sb[:], in_=unit.rearrange("(p t) o -> p (t o)", t=PACK))
         w1_raw = []
         for g in range(PASSES):
             raw = sbuf("w1_raw%d" % g, [P, PACK, H], F32)
             nc.sync.dma_start(out=raw[:], in_=w1[g * P * PACK:(g + 1) * P * PACK, :].rearrange("(p j) n -> p j n", j=PACK))
             w1_raw.append(raw)
-        tables = []
-        for g in range(PASSES):
+
+        def load_table(g):
             table = sbuf("table%d" % g, [P, T], U32)
             nc.sync.dma_start(out=table[:].bitcast(I32), in_=x_words[g].rearrange("p n t -> p (n t)").bitcast(I32))
-            tables.append(table)
-        wo_raw = sbuf("wo_raw", [P, PACK, N], F32)
-        nc.sync.dma_start(out=wo_raw[:], in_=wo.rearrange("(p j) n -> p j n", j=PACK))
+            return table
+
+        tables = [load_table(0)]
 
         identity = sbuf("identity", [P, P], F32)
         make_identity(nc, identity[:])
 
-        picked_rows = sbuf("picked_rows", [P, S], U8)
+        picked_rows = sbuf("picked_rows", [P, S], U8, tag="table1")
         nc.vector.tensor_copy(out=picked_rows[:], in_=scale_rows[:].indirect(offsets[:]))
-        dealt_rows = sbuf("dealt_rows", [P, S], U8)
+        dealt_rows = sbuf("dealt_rows", [P, S], U8, tag="wo_raw")
         nc.vector.tensor_copy(
             out=dealt_rows[:].rearrange("p (b d v) -> p b d v", b=BLOCKS, d=D),
             in_=picked_rows[:].rearrange("p (b v d) -> p b d v", b=BLOCKS, d=D),
         )
-        x_planes = sbuf("x_planes", [P, S], U8)
-        nc.vector.memset(x_planes[:].bitcast(I32), 0)
+        x_planes = []
         for g in range(PASSES):
+            plane = sbuf("x_plane%d" % g, [P, S], U8)
+            nc.vector.memset(plane[:].bitcast(I32), 0)
+            x_planes.append(plane)
+            if g == 1:
+                tables.append(load_table(1))
             for q in range(4):
                 src = 16 * g + 4 * q
-                dst = 32 * q + 4 * g
-                queue = nc.scalar if 4 * g + q < 5 else nc.gpsimd
-                queue.dma_start(out=x_planes[dst:dst + 4, :].bitcast(I32), in_=dealt_rows[src:src + 4, :].bitcast(I32))
+                dst = 32 * q
+                nc.sync.dma_start(out=plane[dst:dst + 4, :].bitcast(I32), in_=dealt_rows[src:src + 4, :].bitcast(I32))
 
-        def quantise_weight(name, raw, width, out_order, in_order):
-            grouped = sbuf(name + "_bf", [P, width, PACK], BF16)
-            nc.scalar.activation(
-                out=grouped[:].rearrange(out_order, i=PACK), in_=raw[:].rearrange(in_order, i=PACK), func=ACT.Copy)
+        wo_raw = sbuf("wo_raw", [P, PACK, N], F32)
+        nc.sync.dma_start(out=wo_raw[:], in_=wo.rearrange("(p j) n -> p j n", j=PACK))
+
+        def quantise(name, grouped, width):
             codes = sbuf(name + "_codes", [P, width], U32)
             plane = sbuf(name + "_plane", [P, width], U8)
             nc.vector.quantize_mx(out=codes[:].bitcast(FP8X4), scales=plane[:], in_=grouped[:].rearrange("p c j -> p (c j)"))
             return codes, plane
 
-        w1_q = [quantise_weight("w1_%d" % g, w1_raw[g], H, "p (i c) j -> p c i j", "p j (c i) -> p c i j") for g in range(PASSES)]
+        w1_q = []
+        for g in range(PASSES):
+            grouped = sbuf("w1_bf%d" % g, [P, H, PACK], BF16)
+            nc.scalar.activation(
+                out=grouped[:].rearrange("p (t m) j -> p m t j", t=PACK),
+                in_=w1_raw[g][:].rearrange("p j (m t) -> p m t j", t=PACK), func=ACT.Copy)
+            w1_q.append(quantise("w1_%d" % g, grouped, H))
 
         y = [[bank("y%d_%d" % (b, d), D * b + d, [P, H]) for d in range(D)] for b in range(BLOCKS)]
         for g in range(PASSES):
@@ -99,19 +108,18 @@ def tile_picked_yhdrmg_dev_p_kernel(tc, x_words, x_scales, w1, logt, unit, wo, o
                     out=picked[:].rearrange("p d v -> p v d"),
                     in_=tables[g][:].indirect(offsets[:, b * cols:(b + 1) * cols]),
                 )
-                for d in range(D):
+                for d in (1, 0, 2, 3):
                     first = b * ENTRIES + d * P
                     nc.tensor.matmul_mx(
                         out=y[b][d][:],
                         lhsT=picked[:, d, :].bitcast(FP8X4),
-                        lhsT_scale=x_planes[4 * g:P, first:first + P],
+                        lhsT_scale=x_planes[g][:, first:first + P],
                         rhs=w1_q[g][0][:].bitcast(FP8X4),
                         rhs_scale=w1_q[g][1][:],
                         start=(g == 0),
                         stop=(g == PASSES - 1),
                     )
 
-        wo_codes, wo_plane = quantise_weight("wo", wo_raw, N, "p (c i) j -> p c j i", "p j (c i) -> p c j i")
 
         def turned_add(total, term, start, stop):
             for t in range(PACK):
@@ -120,52 +128,78 @@ def tile_picked_yhdrmg_dev_p_kernel(tc, x_words, x_scales, w1, logt, unit, wo, o
                     start=(start and t == 0), stop=(stop and t == PACK - 1), is_transpose=True,
                 )
 
+        wide = [P, PACK, P]
+        yb = [[y[b][d][:].rearrange("p (t m) -> p t m", t=PACK) for d in range(D)] for b in range(BLOCKS)]
+        pairs = [[sbuf("tanh%d_%d" % (b, u), [P, 2, PACK, P], F32) for u in range(2)] for b in range(BLOCKS)]
+        th = [[pairs[b][d // 2][:, d % 2] for d in range(D)] for b in range(BLOCKS)]
+        sq = [[sbuf("sq%d_%d" % (b, d), wide, F32) for d in range(D)] for b in range(BLOCKS)]
+        base = [sbuf("base%d" % b, wide, F32) for b in range(BLOCKS)]
+
+        def first_member(b):
+            nc.vector.tensor_scalar(out=base[b][:], in0=yb[b][0], scalar1=log_time[:, b, 0:1], scalar2=None, op0=ALU.subtract)
+            nc.scalar.activation(out=th[b][0], in_=yb[b][0], func=ACT.Tanh, scale=0.5)
+
+        def first_square(b):
+            nc.vector.scalar_tensor_tensor(
+                out=sq[b][0][:], in0=th[b][0], scalar=TANH_GAIN * TANH_GAIN, in1=th[b][0], op0=ALU.mult, op1=ALU.mult)
+
+        def weight(b, d):
+            nc.scalar.activation(out=th[b][d], in_=yb[b][d], func=ACT.Tanh, scale=0.5)
+            nc.scalar.activation(out=sq[b][d][:], in_=th[b][d], func=ACT.Square, scale=TANH_GAIN)
+
+        firsts = [[sbuf("first%d_%d" % (b, d), wide, F32) for d in range(1, D)] for b in range(BLOCKS)]
+        seconds = [[sbuf("second%d_%d" % (b, d), wide, F32) for d in range(1, D)] for b in range(BLOCKS)]
+
+        def moments(b, d):
+            dev = sbuf("dev%d_%d" % (b, d), wide, F32)
+            nc.vector.scalar_tensor_tensor(
+                out=dev[:], in0=yb[b][d], scalar=log_time[:, b, d:d + 1], in1=base[b][:], op0=ALU.subtract, op1=ALU.subtract)
+            nc.vector.scalar_tensor_tensor(
+                out=firsts[b][d - 1][:], in0=sq[b][d][:], scalar=PEAK, in1=dev[:], op0=ALU.subtract, op1=ALU.mult)
+            nc.vector.tensor_tensor(out=seconds[b][d - 1][:], in0=firsts[b][d - 1][:], in1=dev[:], op=ALU.mult)
+
+        def add_up(name, index, terms):
+            total = bank(name, index, wide)
+            for n, term in enumerate(terms):
+                turned_add(total, term, n == 0, n == len(terms) - 1)
+            return total[:].rearrange("p t v -> p v t")
+
+        weight(0, 1)
+        first_member(0)
+        moments(0, 1)
+        first_square(0)
+        weight(0, 2)
+        moments(0, 2)
+        weight(0, 3)
+        first_member(1)
+        first_square(1)
+        sq_sums = [add_up("sq_sum0", 0, [sq[0][d] for d in (1, 0, 2, 3)])]
+        moments(0, 3)
+        for d in range(1, D):
+            weight(1, d)
+        sq_sums.append(add_up("sq_sum1", D, sq[1]))
         sums = []
         for b in range(BLOCKS):
-            yb = [y[b][d][:].rearrange("p (t m) -> p t m", t=PACK) for d in range(D)]
-            pairs = [sbuf("tanh%d_%d" % (b, u), [P, 2, PACK, P], F32) for u in range(2)]
-            th = [pairs[d // 2][:, d % 2] for d in range(D)]
-            sq = [sbuf("sq%d_%d" % (b, d), [P, PACK, P], F32) for d in range(D)]
-            base = sbuf("base%d" % b, [P, PACK, P], F32)
-            nc.vector.tensor_scalar(out=base[:], in0=yb[0], scalar1=log_time[:, b, 0:1], scalar2=None, op0=ALU.subtract)
-            firsts, seconds = [], []
-            for d in range(1, D):
-                nc.scalar.activation(out=th[d], in_=yb[d], func=ACT.Tanh, scale=0.5)
-                nc.scalar.activation(out=sq[d][:], in_=th[d], func=ACT.Square, scale=TANH_GAIN)
-                dev = sbuf("dev%d_%d" % (b, d), [P, PACK, P], F32)
-                nc.vector.scalar_tensor_tensor(
-                    out=dev[:], in0=yb[d], scalar=log_time[:, b, d:d + 1], in1=base[:], op0=ALU.subtract, op1=ALU.subtract)
-                if d == 1:
-                    nc.scalar.activation(out=th[0], in_=yb[0], func=ACT.Tanh, scale=0.5)
-                m1 = sbuf("first%d_%d" % (b, d), [P, PACK, P], F32)
-                nc.vector.scalar_tensor_tensor(
-                    out=m1[:], in0=sq[d][:], scalar=PEAK, in1=dev[:], op0=ALU.subtract, op1=ALU.mult)
-                m2 = sbuf("second%d_%d" % (b, d), [P, PACK, P], F32)
-                nc.vector.tensor_tensor(out=m2[:], in0=m1[:], in1=dev[:], op=ALU.mult)
-                if d == 1:
-                    nc.vector.scalar_tensor_tensor(
-                        out=sq[0][:], in0=th[0], scalar=TANH_GAIN * TANH_GAIN, in1=th[0], op0=ALU.mult, op1=ALU.mult)
-                firsts.append(m1)
-                seconds.append(m2)
-            sq_sum = bank("sq_sum%d" % b, D * b, [P, PACK, P])
-            for n, d in enumerate((1, 0, 2, 3)):
-                turned_add(sq_sum, sq[d], n == 0, n == D - 1)
-            base_t = bank("base_t%d" % b, D * b + 1, [P, PACK, P])
-            turned_add(base_t, base, True, True)
-            first_sum = bank("first_sum%d" % b, D * b + 2, [P, PACK, P])
-            second_sum = bank("second_sum%d" % b, D * b + 3, [P, PACK, P])
-            for n in range(D - 1):
-                turned_add(first_sum, firsts[n], n == 0, n == D - 2)
-            for n in range(D - 1):
-                turned_add(second_sum, seconds[n], n == 0, n == D - 2)
-            sums.append([tile[:].rearrange("p t v -> p v t") for tile in (sq_sum, base_t, first_sum, second_sum)])
+            if b == 1:
+                for d in range(1, D):
+                    moments(1, d)
+            sums.append([
+                sq_sums[b],
+                add_up("base_t%d" % b, D * b + 1, [base[b]]),
+                add_up("first_sum%d" % b, D * b + 2, firsts[b]),
+                add_up("second_sum%d" % b, D * b + 3, seconds[b]),
+            ])
 
         shape = [P, BLOCKS, P, PACK]
         log_den = sbuf("log_den", shape, F32, tag="tanh%d_1" % (BLOCKS - 1))
         for b in range(BLOCKS):
             nc.scalar.activation(out=log_den[:, b], in_=sums[b][0], func=ACT.Ln, scale=-1.0, bias=D * PEAK - 1.0)
         recip = sbuf("recip", shape, F32)
-        nc.scalar.activation(out=recip[:], in_=log_den[:], func=ACT.Sigmoid, scale=-1.0)
+        flat_log = log_den[:].rearrange("p b v t -> p (b v t)")
+        flat_recip = recip[:].rearrange("p b v t -> p (b v t)")
+        cut = P * PACK + 64
+        for lo, hi in ((0, cut), (cut, BLOCKS * P * PACK)):
+            nc.scalar.activation(out=flat_recip[:, lo:hi], in_=flat_log[:, lo:hi], func=ACT.Sigmoid, scale=-1.0)
         half = [P, P, PACK]
         means, mean_sqs, bounded = [], [], []
         for b in range(BLOCKS):
@@ -179,6 +213,10 @@ def tile_picked_yhdrmg_dev_p_kernel(tc, x_words, x_scales, w1, logt, unit, wo, o
             nc.scalar.activation(out=bound[:], in_=rad[:], func=ACT.Tanh)
             mean_sqs.append(mean_sq)
             bounded.append(bound)
+        wo_bf = sbuf("wo_bf", [P, N, PACK], BF16)
+        nc.gpsimd.tensor_scalar(
+            out=wo_bf[:], in0=wo_raw[:].rearrange("p j c -> p c j"), scalar1=1.0, scalar2=0.0, op0=ALU.mult, op1=ALU.add)
+        wo_codes, wo_plane = quantise("wo", wo_bf, N)
         variances = []
         for b in range(BLOCKS):
             raw_second = sbuf("raw_second%d" % b, half, F32)

@@ -65,7 +65,7 @@ def tile_picked_yhdrmg_dev_p_kernel(tc, x_words, x_scales, w1, logt, unit, wo, o
 
         picked_rows = sbuf("picked_rows", [P, S], U8, tag="table1")
         nc.vector.tensor_copy(out=picked_rows[:], in_=scale_rows[:].indirect(offsets[:]))
-        dealt_rows = sbuf("dealt_rows", [P, S], U8, tag="wo_raw")
+        dealt_rows = sbuf("dealt_rows", [P, S], U8)
         nc.vector.tensor_copy(
             out=dealt_rows[:].rearrange("p (b d v) -> p b d v", b=BLOCKS, d=D),
             in_=picked_rows[:].rearrange("p (b v d) -> p b d v", b=BLOCKS, d=D),
@@ -75,15 +75,13 @@ def tile_picked_yhdrmg_dev_p_kernel(tc, x_words, x_scales, w1, logt, unit, wo, o
             plane = sbuf("x_plane%d" % g, [P, S], U8)
             nc.vector.memset(plane[:].bitcast(I32), 0)
             x_planes.append(plane)
-            if g == 1:
-                tables.append(load_table(1))
             for q in range(4):
                 src = 16 * g + 4 * q
                 dst = 32 * q
-                nc.sync.dma_start(out=plane[dst:dst + 4, :].bitcast(I32), in_=dealt_rows[src:src + 4, :].bitcast(I32))
+                queue = nc.sync if 4 * g + q < 6 else nc.gpsimd
+                queue.dma_start(out=plane[dst:dst + 4, :].bitcast(I32), in_=dealt_rows[src:src + 4, :].bitcast(I32))
 
-        wo_raw = sbuf("wo_raw", [P, PACK, N], F32)
-        nc.sync.dma_start(out=wo_raw[:], in_=wo.rearrange("(p j) n -> p j n", j=PACK))
+        tables.append(load_table(1))
 
         def quantise(name, grouped, width):
             codes = sbuf(name + "_codes", [P, width], U32)
@@ -98,6 +96,13 @@ def tile_picked_yhdrmg_dev_p_kernel(tc, x_words, x_scales, w1, logt, unit, wo, o
                 out=grouped[:].rearrange("p (t m) j -> p m t j", t=PACK),
                 in_=w1_raw[g][:].rearrange("p j (m t) -> p m t j", t=PACK), func=ACT.Copy)
             w1_q.append(quantise("w1_%d" % g, grouped, H))
+
+        wo_raw = sbuf("wo_raw", [P, PACK, N], F32, tag="w1_raw0")
+        nc.sync.dma_start(out=wo_raw[:], in_=wo.rearrange("(p j) n -> p j n", j=PACK))
+
+        wo_bf = sbuf("wo_bf", [P, N, PACK], BF16)
+        nc.scalar.activation(
+            out=wo_bf[:].rearrange("p (c i) j -> p c j i", i=4), in_=wo_raw[:].rearrange("p j (c i) -> p c j i", i=4), func=ACT.Copy)
 
         y = [[bank("y%d_%d" % (b, d), D * b + d, [P, H]) for d in range(D)] for b in range(BLOCKS)]
         for g in range(PASSES):
@@ -135,28 +140,34 @@ def tile_picked_yhdrmg_dev_p_kernel(tc, x_words, x_scales, w1, logt, unit, wo, o
         sq = [[sbuf("sq%d_%d" % (b, d), wide, F32) for d in range(D)] for b in range(BLOCKS)]
         base = [sbuf("base%d" % b, wide, F32) for b in range(BLOCKS)]
 
-        def first_member(b):
-            nc.vector.tensor_scalar(out=base[b][:], in0=yb[b][0], scalar1=log_time[:, b, 0:1], scalar2=None, op0=ALU.subtract)
-            nc.scalar.activation(out=th[b][0], in_=yb[b][0], func=ACT.Tanh, scale=0.5)
-
-        def first_square(b):
-            nc.vector.scalar_tensor_tensor(
-                out=sq[b][0][:], in0=th[b][0], scalar=TANH_GAIN * TANH_GAIN, in1=th[b][0], op0=ALU.mult, op1=ALU.mult)
-
-        def weight(b, d):
-            nc.scalar.activation(out=th[b][d], in_=yb[b][d], func=ACT.Tanh, scale=0.5)
-            nc.scalar.activation(out=sq[b][d][:], in_=th[b][d], func=ACT.Square, scale=TANH_GAIN)
-
+        devs = [[sbuf("dev%d_%d" % (b, d), wide, F32) for d in range(1, D)] for b in range(BLOCKS)]
         firsts = [[sbuf("first%d_%d" % (b, d), wide, F32) for d in range(1, D)] for b in range(BLOCKS)]
         seconds = [[sbuf("second%d_%d" % (b, d), wide, F32) for d in range(1, D)] for b in range(BLOCKS)]
 
-        def moments(b, d):
-            dev = sbuf("dev%d_%d" % (b, d), wide, F32)
+        def tanh_half(b, d):
+            nc.scalar.activation(out=th[b][d], in_=yb[b][d], func=ACT.Tanh, scale=0.5)
+
+        def square(b, d):
+            if d == 0:
+                nc.vector.scalar_tensor_tensor(
+                    out=sq[b][0][:], in0=th[b][0], scalar=TANH_GAIN * TANH_GAIN, in1=th[b][0], op0=ALU.mult, op1=ALU.mult)
+            else:
+                nc.scalar.activation(out=sq[b][d][:], in_=th[b][d], func=ACT.Square, scale=TANH_GAIN)
+
+        def deviation(b, d):
+            if d == 0:
+                nc.vector.tensor_scalar(out=base[b][:], in0=yb[b][0], scalar1=log_time[:, b, 0:1], scalar2=None, op0=ALU.subtract)
+            else:
+                nc.vector.scalar_tensor_tensor(
+                    out=devs[b][d - 1][:], in0=yb[b][d], scalar=log_time[:, b, d:d + 1], in1=base[b][:],
+                    op0=ALU.subtract, op1=ALU.subtract)
+
+        def first(b, d):
             nc.vector.scalar_tensor_tensor(
-                out=dev[:], in0=yb[b][d], scalar=log_time[:, b, d:d + 1], in1=base[b][:], op0=ALU.subtract, op1=ALU.subtract)
-            nc.vector.scalar_tensor_tensor(
-                out=firsts[b][d - 1][:], in0=sq[b][d][:], scalar=PEAK, in1=dev[:], op0=ALU.subtract, op1=ALU.mult)
-            nc.vector.tensor_tensor(out=seconds[b][d - 1][:], in0=firsts[b][d - 1][:], in1=dev[:], op=ALU.mult)
+                out=firsts[b][d - 1][:], in0=sq[b][d][:], scalar=PEAK, in1=devs[b][d - 1][:], op0=ALU.subtract, op1=ALU.mult)
+
+        def second(b, d):
+            nc.vector.tensor_tensor(out=seconds[b][d - 1][:], in0=firsts[b][d - 1][:], in1=devs[b][d - 1][:], op=ALU.mult)
 
         def add_up(name, index, terms):
             total = bank(name, index, wide)
@@ -164,25 +175,46 @@ def tile_picked_yhdrmg_dev_p_kernel(tc, x_words, x_scales, w1, logt, unit, wo, o
                 turned_add(total, term, n == 0, n == len(terms) - 1)
             return total[:].rearrange("p t v -> p v t")
 
-        weight(0, 1)
-        first_member(0)
-        moments(0, 1)
-        first_square(0)
-        weight(0, 2)
-        moments(0, 2)
-        weight(0, 3)
-        first_member(1)
-        first_square(1)
-        sq_sums = [add_up("sq_sum0", 0, [sq[0][d] for d in (1, 0, 2, 3)])]
-        moments(0, 3)
-        for d in range(1, D):
-            weight(1, d)
-        sq_sums.append(add_up("sq_sum1", D, sq[1]))
+        tanh_half(0, 1)
+        deviation(0, 0)
+        tanh_half(0, 2)
+        square(0, 1)
+        deviation(0, 1)
+        deviation(0, 2)
+        tanh_half(0, 0)
+        square(0, 2)
+        first(0, 1)
+        square(0, 0)
+        second(0, 1)
+        tanh_half(0, 3)
+        tanh_half(1, 0)
+        square(0, 3)
+        first(0, 2)
+        deviation(0, 3)
+        second(0, 2)
+        sq_sums = [add_up("sq_sum0", 0, [sq[0][d] for d in (1, 2, 0, 3)])]
+        tanh_half(1, 1)
+        tanh_half(1, 2)
+        square(1, 1)
+        tanh_half(1, 3)
+        square(1, 2)
+        square(1, 3)
+        deviation(1, 0)
+        first(0, 3)
+        square(1, 0)
+        second(0, 3)
+        sq_sums.append(add_up("sq_sum1", D, [sq[1][d] for d in (1, 2, 0, 3)]))
+        deviation(1, 1)
+        deviation(1, 2)
+        first(1, 1)
+        deviation(1, 3)
+        second(1, 1)
+        first(1, 2)
+        first(1, 3)
+        second(1, 2)
+        second(1, 3)
         sums = []
         for b in range(BLOCKS):
-            if b == 1:
-                for d in range(1, D):
-                    moments(1, d)
             sums.append([
                 sq_sums[b],
                 add_up("base_t%d" % b, D * b + 1, [base[b]]),
@@ -201,40 +233,33 @@ def tile_picked_yhdrmg_dev_p_kernel(tc, x_words, x_scales, w1, logt, unit, wo, o
         for lo, hi in ((0, cut), (cut, BLOCKS * P * PACK)):
             nc.scalar.activation(out=flat_recip[:, lo:hi], in_=flat_log[:, lo:hi], func=ACT.Sigmoid, scale=-1.0)
         half = [P, P, PACK]
-        means, mean_sqs, bounded = [], [], []
-        for b in range(BLOCKS):
-            mean = sbuf("mean%d" % b, half, F32)
-            nc.vector.scalar_tensor_tensor(out=mean[:], in0=sums[b][2], scalar=-1.0, in1=recip[:, b], op0=ALU.mult, op1=ALU.mult)
-            rad = sbuf("rad%d" % b, half, F32)
-            nc.vector.tensor_tensor(out=rad[:], in0=sums[b][1], in1=mean[:], op=ALU.add)
-            mean_sq = sbuf("mean_sq%d" % b, half, F32)
-            nc.scalar.activation(out=mean_sq[:], in_=mean[:], func=ACT.Square)
-            bound = sbuf("bounded%d" % b, half, F32)
-            nc.scalar.activation(out=bound[:], in_=rad[:], func=ACT.Tanh)
-            mean_sqs.append(mean_sq)
-            bounded.append(bound)
-        wo_bf = sbuf("wo_bf", [P, N, PACK], BF16)
-        nc.gpsimd.tensor_scalar(
-            out=wo_bf[:], in0=wo_raw[:].rearrange("p j c -> p c j"), scalar1=1.0, scalar2=0.0, op0=ALU.mult, op1=ALU.add)
+        blocks = range(BLOCKS)
+
+        def per_block(name, dtype=F32):
+            return [sbuf("%s%d" % (name, b), half, dtype) for b in blocks]
+
         wo_codes, wo_plane = quantise("wo", wo_bf, N)
-        variances = []
-        for b in range(BLOCKS):
-            raw_second = sbuf("raw_second%d" % b, half, F32)
-            nc.vector.scalar_tensor_tensor(out=raw_second[:], in0=sums[b][3], scalar=-1.0, in1=recip[:, b], op0=ALU.mult, op1=ALU.mult)
-            var = sbuf("var%d" % b, half, F32)
-            nc.vector.tensor_tensor(out=var[:], in0=raw_second[:], in1=mean_sqs[b][:], op=ALU.subtract)
-            variances.append(var)
-        for b in range(BLOCKS):
-            gained = sbuf("gained%d" % b, half, F32)
+        mean, mean_sq, rad, bounded = per_block("mean"), per_block("mean_sq"), per_block("rad"), per_block("bounded")
+        raw_second, var, gained, zz = per_block("raw_second"), per_block("var"), per_block("gained"), per_block("zz", BF16)
+        for b in blocks:
+            nc.vector.scalar_tensor_tensor(out=mean[b][:], in0=sums[b][2], scalar=-1.0, in1=recip[:, b], op0=ALU.mult, op1=ALU.mult)
+            nc.scalar.activation(out=mean_sq[b][:], in_=mean[b][:], func=ACT.Square)
+        for b in blocks:
+            nc.vector.tensor_tensor(out=rad[b][:], in0=sums[b][1], in1=mean[b][:], op=ALU.add)
+            nc.scalar.activation(out=bounded[b][:], in_=rad[b][:], func=ACT.Tanh)
+        for b in blocks:
+            nc.vector.scalar_tensor_tensor(out=raw_second[b][:], in0=sums[b][3], scalar=-1.0, in1=recip[:, b], op0=ALU.mult, op1=ALU.mult)
+        for b in blocks:
+            nc.vector.tensor_tensor(out=var[b][:], in0=raw_second[b][:], in1=mean_sq[b][:], op=ALU.subtract)
+        for b in blocks:
             nc.vector.tensor_tensor(
-                out=gained[:], in0=bounded[b][:], in1=unit_sb[:].unsqueeze(1).to_broadcast(half), op=ALU.mult)
+                out=gained[b][:], in0=bounded[b][:], in1=unit_sb[:].unsqueeze(1).to_broadcast(half), op=ALU.mult)
+        for b in blocks:
             spread = sbuf("spread%d" % b, half, F32, tag="rad%d" % (BLOCKS - 1 - b))
-            nc.scalar.activation(out=spread[:], in_=variances[b][:], func=ACT.Sqrt)
-            zz = sbuf("zz%d" % b, half, BF16)
-            nc.vector.tensor_tensor(out=zz[:], in0=gained[:], in1=spread[:], op=ALU.mult)
-            z_codes = sbuf("z_codes%d" % b, [P, P], U32)
-            z_plane = sbuf("z_plane%d" % b, [P, P], U8)
-            nc.vector.quantize_mx(out=z_codes[:].bitcast(FP8X4), scales=z_plane[:], in_=zz[:].rearrange("p v t -> p (v t)"))
+            nc.scalar.activation(out=spread[:], in_=var[b][:], func=ACT.Sqrt)
+            nc.vector.tensor_tensor(out=zz[b][:], in0=gained[b][:], in1=spread[:], op=ALU.mult)
+        for b in blocks:
+            z_codes, z_plane = quantise("z%d" % b, zz[b], P)
             acc = bank("acc%d" % b, D * b, [P, P])
             nc.tensor.matmul_mx(
                 out=acc[:], lhsT=wo_codes[:].bitcast(FP8X4), lhsT_scale=wo_plane[:],

from contextlib import ExitStack

import concourse.mybir as mybir
from concourse.masks import make_identity

H, K, T, S, D, N = 512, 1024, 4096, 1024, 4, 128
FLOPS = 2 * K * H * S + 2 * H * N * (S // D)

F32 = mybir.dt.float32
BF16 = mybir.dt.bfloat16
I32 = mybir.dt.int32
U32 = mybir.dt.uint32
U16 = mybir.dt.uint16
U8 = mybir.dt.uint8
FP8X4 = mybir.dt.float8_e4m3fn_x4
ACT = mybir.ActivationFunctionType
ALU = mybir.AluOpType

P = 128
PACK = 4
PASSES = K // (P * PACK)
BLOCKS = S // (D * P)
ENTRIES = D * P
TANH_GAIN = 2.5
PEAK = 6.75


def tile_picked_yhdrmg_dev_p_kernel(tc, x_words, x_scales, w1, logt, unit, wo, offs, out):
    nc = tc.nc
    with ExitStack() as ctx:
        keep = ctx.enter_context(tc.tile_pool(name="keep", bufs=1))
        psum = ctx.enter_context(tc.psum_pool(name="psum", bufs=1))

        def sbuf(name, shape, dtype, tag=None):
            return keep.tile(shape, dtype, name=name, tag=tag or name, align_bytes=64)

        def bank(name, index, shape):
            return psum.tile(shape, F32, name=name, tag="bank%d" % index)

        offsets = keep.tile([P, S // 16], U16, name="offsets")
        nc.sync.dma_start(offsets[:], offs)
        scale_rows = sbuf("scale_rows", [P, T], U8)
        nc.sync.dma_start(out=scale_rows[0:32, :].bitcast(I32), in_=x_scales.rearrange("o q c -> (o q) c").bitcast(I32))
        nc.vector.memset(scale_rows[32:64, :].bitcast(I32), 0)
        nc.vector.memset(scale_rows[64:128, :].bitcast(I32), 0)
        log_time = sbuf("log_time", [P, BLOCKS, D], F32)
        nc.gpsimd.dma_start(out=log_time[:], in_=logt[0].rearrange("(b p d) -> p b d", b=BLOCKS, d=D))
        unit_sb = sbuf("unit_sb", [P, PACK], F32)
        nc.gpsimd.dma_start(out=unit_sb[:], in_=unit.rearrange("(p t) o -> p (t o)", t=PACK))
        w1_raw = []
        for g in range(PASSES):
            raw = sbuf("w1_raw%d" % g, [P, PACK, H], F32)
            nc.sync.dma_start(out=raw[:], in_=w1[g * P * PACK:(g + 1) * P * PACK, :].rearrange("(p j) n -> p j n", j=PACK))
            w1_raw.append(raw)

        def load_table(g):
            table = sbuf("table%d" % g, [P, T], U32)
            nc.sync.dma_start(out=table[:].bitcast(I32), in_=x_words[g].rearrange("p n t -> p (n t)").bitcast(I32))
            return table

        tables = [load_table(0)]

        identity = sbuf("identity", [P, P], F32)
        make_identity(nc, identity[:])

        picked_rows = sbuf("picked_rows", [P, S], U8, tag="table1")
        nc.vector.tensor_copy(out=picked_rows[:], in_=scale_rows[:].indirect(offsets[:]))
        dealt_rows = sbuf("dealt_rows", [P, S], U8)
        nc.vector.tensor_copy(
            out=dealt_rows[:].rearrange("p (b d v) -> p b d v", b=BLOCKS, d=D),
            in_=picked_rows[:].rearrange("p (b v d) -> p b d v", b=BLOCKS, d=D),
        )
        x_planes = []
        for g in range(PASSES):
            plane = sbuf("x_plane%d" % g, [P, S], U8)
            nc.vector.memset(plane[:].bitcast(I32), 0)
            x_planes.append(plane)
            for q in range(4):
                src = 16 * g + 4 * q
                dst = 32 * q
                queue = nc.sync if 4 * g + q < 6 else nc.gpsimd
                queue.dma_start(out=plane[dst:dst + 4, :].bitcast(I32), in_=dealt_rows[src:src + 4, :].bitcast(I32))

        tables.append(load_table(1))

        def quantise(name, grouped, width):
            codes = sbuf(name + "_codes", [P, width], U32)
            plane = sbuf(name + "_plane", [P, width], U8)
            nc.vector.quantize_mx(out=codes[:].bitcast(FP8X4), scales=plane[:], in_=grouped[:].rearrange("p c j -> p (c j)"))
            return codes, plane

        w1_q = []
        for g in range(PASSES):
            grouped = sbuf("w1_bf%d" % g, [P, H, PACK], BF16)
            nc.scalar.activation(
                out=grouped[:].rearrange("p (t m) j -> p m t j", t=PACK),
                in_=w1_raw[g][:].rearrange("p j (m t) -> p m t j", t=PACK), func=ACT.Copy)
            w1_q.append(quantise("w1_%d" % g, grouped, H))

        wo_raw = sbuf("wo_raw", [P, PACK, N], F32, tag="w1_raw0")
        nc.sync.dma_start(out=wo_raw[:], in_=wo.rearrange("(p j) n -> p j n", j=PACK))

        wo_bf = sbuf("wo_bf", [P, N, PACK], BF16)
        nc.scalar.activation(
            out=wo_bf[:].rearrange("p (c i) j -> p c j i", i=4), in_=wo_raw[:].rearrange("p j (c i) -> p c j i", i=4), func=ACT.Copy)

        y = [[bank("y%d_%d" % (b, d), D * b + d, [P, H]) for d in range(D)] for b in range(BLOCKS)]
        for g in range(PASSES):
            for b in range(BLOCKS):
                picked = sbuf("picked%d_%d" % (g, b), [P, D, P], U32)
                cols = ENTRIES // 16
                nc.vector.tensor_copy(
                    out=picked[:].rearrange("p d v -> p v d"),
                    in_=tables[g][:].indirect(offsets[:, b * cols:(b + 1) * cols]),
                )
                for d in (1, 0, 2, 3):
                    first = b * ENTRIES + d * P
                    nc.tensor.matmul_mx(
                        out=y[b][d][:],
                        lhsT=picked[:, d, :].bitcast(FP8X4),
                        lhsT_scale=x_planes[g][:, first:first + P],
                        rhs=w1_q[g][0][:].bitcast(FP8X4),
                        rhs_scale=w1_q[g][1][:],
                        start=(g == 0),
                        stop=(g == PASSES - 1),
                    )


        def turned_add(total, term, start, stop):
            for t in range(PACK):
                nc.tensor.matmul(
                    total[:, t, :], lhsT=term[:, t, :], rhs=identity[:],
                    start=(start and t == 0), stop=(stop and t == PACK - 1), is_transpose=True,
                )

        wide = [P, PACK, P]
        yb = [[y[b][d][:].rearrange("p (t m) -> p t m", t=PACK) for d in range(D)] for b in range(BLOCKS)]
        pairs = [[sbuf("tanh%d_%d" % (b, u), [P, 2, PACK, P], F32) for u in range(2)] for b in range(BLOCKS)]
        th = [[pairs[b][d // 2][:, d % 2] for d in range(D)] for b in range(BLOCKS)]
        sq = [[sbuf("sq%d_%d" % (b, d), wide, F32) for d in range(D)] for b in range(BLOCKS)]
        base = [sbuf("base%d" % b, wide, F32) for b in range(BLOCKS)]

        devs = [[sbuf("dev%d_%d" % (b, d), wide, F32) for d in range(1, D)] for b in range(BLOCKS)]
        firsts = [[sbuf("first%d_%d" % (b, d), wide, F32) for d in range(1, D)] for b in range(BLOCKS)]
        seconds = [[sbuf("second%d_%d" % (b, d), wide, F32) for d in range(1, D)] for b in range(BLOCKS)]

        def tanh_half(b, d):
            nc.scalar.activation(out=th[b][d], in_=yb[b][d], func=ACT.Tanh, scale=0.5)

        def square(b, d):
            if d == 0:
                nc.vector.scalar_tensor_tensor(
                    out=sq[b][0][:], in0=th[b][0], scalar=TANH_GAIN * TANH_GAIN, in1=th[b][0], op0=ALU.mult, op1=ALU.mult)
            else:
                nc.scalar.activation(out=sq[b][d][:], in_=th[b][d], func=ACT.Square, scale=TANH_GAIN)

        def deviation(b, d):
            if d == 0:
                nc.vector.tensor_scalar(out=base[b][:], in0=yb[b][0], scalar1=log_time[:, b, 0:1], scalar2=None, op0=ALU.subtract)
            else:
                nc.vector.scalar_tensor_tensor(
                    out=devs[b][d - 1][:], in0=yb[b][d], scalar=log_time[:, b, d:d + 1], in1=base[b][:],
                    op0=ALU.subtract, op1=ALU.subtract)

        def first(b, d):
            nc.vector.scalar_tensor_tensor(
                out=firsts[b][d - 1][:], in0=sq[b][d][:], scalar=PEAK, in1=devs[b][d - 1][:], op0=ALU.subtract, op1=ALU.mult)

        def second(b, d):
            nc.vector.tensor_tensor(out=seconds[b][d - 1][:], in0=firsts[b][d - 1][:], in1=devs[b][d - 1][:], op=ALU.mult)

        def add_up(name, index, terms):
            total = bank(name, index, wide)
            for n, term in enumerate(terms):
                turned_add(total, term, n == 0, n == len(terms) - 1)
            return total[:].rearrange("p t v -> p v t")

        tanh_half(0, 1)
        deviation(0, 0)
        tanh_half(0, 2)
        square(0, 1)
        deviation(0, 1)
        deviation(0, 2)
        tanh_half(0, 0)
        square(0, 2)
        first(0, 1)
        square(0, 0)
        second(0, 1)
        tanh_half(0, 3)
        tanh_half(1, 0)
        square(0, 3)
        first(0, 2)
        deviation(0, 3)
        second(0, 2)
        sq_sums = [add_up("sq_sum0", 0, [sq[0][d] for d in (1, 2, 0, 3)])]
        tanh_half(1, 1)
        tanh_half(1, 2)
        square(1, 1)
        tanh_half(1, 3)
        square(1, 2)
        square(1, 3)
        deviation(1, 0)
        first(0, 3)
        square(1, 0)
        second(0, 3)
        sq_sums.append(add_up("sq_sum1", D, [sq[1][d] for d in (1, 2, 0, 3)]))
        deviation(1, 1)
        deviation(1, 2)
        first(1, 1)
        deviation(1, 3)
        second(1, 1)
        first(1, 2)
        first(1, 3)
        second(1, 2)
        second(1, 3)
        sums = []
        for b in range(BLOCKS):
            sums.append([
                sq_sums[b],
                add_up("base_t%d" % b, D * b + 1, [base[b]]),
                add_up("first_sum%d" % b, D * b + 2, firsts[b]),
                add_up("second_sum%d" % b, D * b + 3, seconds[b]),
            ])

        shape = [P, BLOCKS, P, PACK]
        log_den = sbuf("log_den", shape, F32, tag="tanh%d_1" % (BLOCKS - 1))
        for b in range(BLOCKS):
            nc.scalar.activation(out=log_den[:, b], in_=sums[b][0], func=ACT.Ln, scale=-1.0, bias=D * PEAK - 1.0)
        recip = sbuf("recip", shape, F32)
        flat_log = log_den[:].rearrange("p b v t -> p (b v t)")
        flat_recip = recip[:].rearrange("p b v t -> p (b v t)")
        cut = P * PACK + 64
        for lo, hi in ((0, cut), (cut, BLOCKS * P * PACK)):
            nc.scalar.activation(out=flat_recip[:, lo:hi], in_=flat_log[:, lo:hi], func=ACT.Sigmoid, scale=-1.0)
        half = [P, P, PACK]
        blocks = range(BLOCKS)

        def per_block(name, dtype=F32):
            return [sbuf("%s%d" % (name, b), half, dtype) for b in blocks]

        wo_codes, wo_plane = quantise("wo", wo_bf, N)
        mean, mean_sq, rad, bounded = per_block("mean"), per_block("mean_sq"), per_block("rad"), per_block("bounded")
        raw_second, var, gained, zz = per_block("raw_second"), per_block("var"), per_block("gained"), per_block("zz", BF16)
        for b in blocks:
            nc.vector.scalar_tensor_tensor(out=mean[b][:], in0=sums[b][2], scalar=-1.0, in1=recip[:, b], op0=ALU.mult, op1=ALU.mult)
            nc.scalar.activation(out=mean_sq[b][:], in_=mean[b][:], func=ACT.Square)
        for b in blocks:
            nc.vector.tensor_tensor(out=rad[b][:], in0=sums[b][1], in1=mean[b][:], op=ALU.add)
            nc.scalar.activation(out=bounded[b][:], in_=rad[b][:], func=ACT.Tanh)
        for b in blocks:
            nc.vector.scalar_tensor_tensor(out=raw_second[b][:], in0=sums[b][3], scalar=-1.0, in1=recip[:, b], op0=ALU.mult, op1=ALU.mult)
        for b in blocks:
            nc.vector.tensor_tensor(out=var[b][:], in0=raw_second[b][:], in1=mean_sq[b][:], op=ALU.subtract)
        for b in blocks:
            nc.vector.tensor_tensor(
                out=gained[b][:], in0=bounded[b][:], in1=unit_sb[:].unsqueeze(1).to_broadcast(half), op=ALU.mult)
        for b in blocks:
            spread = sbuf("spread%d" % b, half, F32, tag="rad%d" % (BLOCKS - 1 - b))
            nc.scalar.activation(out=spread[:], in_=var[b][:], func=ACT.Sqrt)
            nc.vector.tensor_tensor(out=zz[b][:], in0=gained[b][:], in1=spread[:], op=ALU.mult)
        for b in blocks:
            z_codes, z_plane = quantise("z%d" % b, zz[b], P)
            acc = bank("acc%d" % b, D * b, [P, P])
            nc.tensor.matmul_mx(
                out=acc[:], lhsT=wo_codes[:].bitcast(FP8X4), lhsT_scale=wo_plane[:],
                rhs=z_codes[:].bitcast(FP8X4), rhs_scale=z_plane[:], start=True, stop=True)
            result = sbuf("result%d" % b, [P, P], F32)
            nc.scalar.copy(out=result[:], in_=acc[:])
            nc.sync.dma_start(out=out[:, b * P:(b + 1) * P], in_=result[:])
